import numpy as np
import ml_dtypes


def mxq(x, axis, fmt="e4m3"):
    dtype, down = {"e4m3": (ml_dtypes.float8_e4m3fn, 7), "e5m2": (ml_dtypes.float8_e5m2, 14)}[fmt]
    v = np.moveaxis(np.asarray(x, np.float32).astype(ml_dtypes.bfloat16).astype(np.float64), axis, -1)
    blocks = v.reshape(v.shape[:-1] + (-1, 32))
    amax = np.abs(blocks).max(-1, keepdims=True)
    byte = np.maximum(np.where(amax > 0, np.frexp(amax)[1] - 1 + 127, 0) - down, 1)
    scale = np.exp2(byte - 127.0)
    codes = (blocks / scale).astype(np.float32).astype(dtype).astype(np.float64)
    return np.moveaxis((codes * scale).reshape(v.shape), -1, axis)


WIDE = False


def mx_kscale(k):
    if not WIDE:
        return np.ones(k)
    levels = np.array([10, -10, 5, -5, 0])
    if k % 512:
        return np.exp2(np.random.permutation(np.resize(levels, k // 32))).repeat(32)
    a = np.empty((k // 512, 16))
    for p in range(k // 512):
        a[p, :8] = np.random.permutation(np.resize(levels, 8))
        for g in range(8):
            far = levels[np.abs(levels - a[p, g]) >= 10]
            a[p, g + 8] = far[np.random.randint(len(far))]
    return np.exp2(a.ravel()).repeat(32)


def f64(x):
    return np.asarray(x).astype(np.float64)


def striped(idx):
    return np.tile(idx.reshape(-1, 16).T, (8, 1)).astype(np.uint16)


def unstriped(offs):
    return offs[:16].T.reshape(-1).astype(np.int64)


def striped8(idx):
    return np.concatenate([x.reshape(-1, 16).T for x in idx]).astype(np.uint16)


def runs(offs, k):
    lists = np.stack([offs[16 * r : 16 * r + 16].T.reshape(-1) for r in range(8)]).astype(np.int64)
    return lists[np.arange(k) % 512 // 64]


def pack_weight(w):
    k, n = w.shape
    w = f64(np.asarray(w, np.float32).astype(ml_dtypes.bfloat16)).reshape(k // 32, 32, n)
    amax = np.abs(w).max(1)
    byte = np.clip(np.where(amax > 0, np.frexp(amax)[1] - 1 + 127 - 7, 1), 1, 254)
    scaled = (w * np.exp2(127.0 - byte)[:, None, :]).reshape(k, n).astype(np.float32)
    words = np.ascontiguousarray(scaled.reshape(k // 512, 128, 4, n).transpose(0, 1, 3, 2)).astype(ml_dtypes.float8_e4m3fn).view(np.uint8)
    return words, np.ascontiguousarray(byte.astype(np.uint8).reshape(k // 512, 16, n))


def unpack_weight(words, scales):
    g, p, n, _ = words.shape
    vals = np.ascontiguousarray(words).view(ml_dtypes.float8_e4m3fn).astype(np.float64) * np.repeat(np.exp2(scales.astype(np.float64) - 127.0), 8, axis=1)[..., None]
    return vals.transpose(0, 1, 3, 2).reshape(g * 512, n)


def sigmoid(v):
    return 1.0 / (1.0 + np.exp(-np.maximum(v, -700.0)))


K, T, S, N, G, H, U = 512, 2048, 256, 512, 2048, 512, 1024


def setup_inputs():
    n = np.random.standard_normal
    s = mx_kscale(K)[:, None]
    u = mx_kscale(K)
    packed_xT = pack_weight(n((K, T)) * s)
    packed_dT = pack_weight(n((K, G)) / s)
    return {
        "x_words": packed_xT[0],
        "x_scales": packed_xT[1],
        "d_words": packed_dT[0],
        "d_scales": packed_dT[1],
        "mem": n((H, U)).astype(np.float32),
        "gn": (np.random.uniform(0.5, 1.5, (H, 1)) * u[:, None]).astype(np.float32),
        "w1": (n((H, N)) / np.sqrt(H) / u[:, None]).astype(np.float32),
        "offs": striped8(np.random.randint(0, T, (8, S))),
        "k1": striped8(np.random.randint(0, G, (8, H))),
        "n1": striped(np.random.permutation(U)[:S]),
        "n2": striped(np.random.permutation(U)),
    }


def reference(x_words, x_scales, d_words, d_scales, mem, gn, w1, offs, k1, n1, n2):
    old = f64(mem)[:, unstriped(n1)]
    d_k1 = unpack_weight(d_words, d_scales)[np.arange(K)[:, None], runs(k1, K)]
    xq = unpack_weight(x_words, x_scales)[np.arange(K)[:, None], runs(offs, K)]
    h = 0.0625 * (d_k1.T @ xq)
    nw = old + sigmoid(h) * (h - old)
    pg = f64(mem).copy()
    pg[:, unstriped(n1)] = nw
    z = f64(gn) * pg
    h2 = mxq(f64(w1), 0, "e4m3").T @ mxq(z, 0, "e4m3")
    return h2 / (np.abs(h2[:, unstriped(n2)]) + 0.5)

@@ -1,0 +1,169 @@
+from contextlib import ExitStack
+
+import concourse.mybir as mybir
+
+F32 = mybir.dt.float32
+BF16 = mybir.dt.bfloat16
+I32 = mybir.dt.int32
+U32 = mybir.dt.uint32
+U16 = mybir.dt.uint16
+U8 = mybir.dt.uint8
+FP8X4 = mybir.dt.float8_e4m3fn_x4
+ACT = mybir.ActivationFunctionType
+ALU = mybir.AluOpType
+
+P = 128
+PACK = 4
+K, T, S, N, G, H, U = 512, 2048, 256, 512, 2048, 512, 1024
+HALF = U // 2
+FLOPS = 2 * K * H * S + 2 * H * N * U
+
+
+def tile_picked_hpqpagetnorm_none_p_kernel(tc, x_words, x_scales, d_words, d_scales, mem, gn, w1, offs, k1, n1, n2, out):
+    nc = tc.nc
+    with ExitStack() as ctx:
+        lists = ctx.enter_context(tc.tile_pool(name="lists", bufs=1))
+        keep = ctx.enter_context(tc.tile_pool(name="keep", bufs=1))
+        psum = ctx.enter_context(tc.psum_pool(name="psum", bufs=1))
+
+        k1_sb = lists.tile([P, H // 16], U16, name="k1_sb")
+        offs_sb = lists.tile([P, S // 16], U16, name="offs_sb")
+        n1_sb = lists.tile([P, S // 16], U16, name="n1_sb")
+        n2_sb = lists.tile([P, U // 16], U16, name="n2_sb")
+
+        d_byte_table = keep.tile([P, G], U8, name="d_byte_table", align_bytes=64)
+        x_byte_table = keep.tile([P, T], U8, name="x_byte_table", align_bytes=64)
+        nc.vector.memset(d_byte_table[:].bitcast(I32), 0)
+        nc.gpsimd.memset(x_byte_table[:].bitcast(I32), 0)
+        nc.scalar.dma_start(out=d_byte_table[0:P:8, :].bitcast(I32), in_=d_scales[0].bitcast(I32))
+        nc.scalar.dma_start(out=x_byte_table[0:P:8, :].bitcast(I32), in_=x_scales[0].bitcast(I32))
+
+        d_word_table = keep.tile([P, G], I32, name="d_word_table", align_bytes=64)
+        x_word_table = keep.tile([P, T], I32, name="x_word_table", align_bytes=64)
+        nc.sync.dma_start(k1_sb[:], k1)
+        nc.sync.dma_start(offs_sb[:], offs)
+        nc.sync.dma_start(n1_sb[:], n1)
+        nc.sync.dma_start(n2_sb[:], n2)
+        nc.sync.dma_start(out=d_word_table[:], in_=d_words[0].rearrange("p n t -> p (n t)").bitcast(I32))
+        nc.sync.dma_start(out=x_word_table[:], in_=x_words[0].rearrange("p n t -> p (n t)").bitcast(I32))
+        gn_sb = keep.tile([P, PACK], F32, name="gn_sb")
+        nc.gpsimd.dma_start(out=gn_sb[:], in_=gn.rearrange("(p t) o -> p (t o)", t=PACK))
+
+        d_bytes = keep.tile([P, H], U8, name="d_bytes", align_bytes=64)
+        x_bytes = keep.tile([P, S], U8, name="x_bytes", align_bytes=64)
+        dealt_bytes = keep.tile([P, H + S], U8, name="dealt_bytes", align_bytes=64)
+        scale_rows = keep.tile([P, H + S], U8, name="scale_rows", align_bytes=64)
+        nc.vector.tensor_copy(d_bytes[:], d_byte_table[:].indirect(k1_sb[:]))
+        nc.vector.tensor_copy(x_bytes[:], x_byte_table[:].indirect(offs_sb[:]))
+        nc.vector.tensor_copy(out=dealt_bytes[:, 0:H].rearrange("p (t m) -> p t m", t=PACK),
+                              in_=d_bytes[:].rearrange("p (m t) -> p t m", t=PACK))
+        nc.vector.tensor_copy(out=dealt_bytes[:, H:H + S].bitcast(I32), in_=x_bytes[:].bitcast(I32))
+        nc.vector.tensor_copy(out=scale_rows[:].bitcast(I32), in_=dealt_bytes[:].bitcast(I32))
+        for b in range(1, 4):
+            nc.scalar.dma_start(out=scale_rows[b:P:32, :].bitcast(I32), in_=dealt_bytes[8 * b:P:32, :].bitcast(I32))
+
+        d_picked = keep.tile([P, H], U32, name="d_picked", tag="x_byte_table", align_bytes=64)
+        d_dealt = keep.tile([P, H], U32, name="d_dealt", align_bytes=64)
+        x_picked = keep.tile([P, S], U32, name="x_picked", align_bytes=64)
+        nc.vector.tensor_copy(d_picked[:], d_word_table[:].bitcast(U32).indirect(k1_sb[:]))
+        nc.vector.tensor_copy(out=d_dealt[:].rearrange("p (t m) -> p t m", t=PACK),
+                              in_=d_picked[:].rearrange("p (m t) -> p t m", t=PACK))
+        nc.vector.tensor_copy(x_picked[:], x_word_table[:].bitcast(U32).indirect(offs_sb[:]))
+
+        mem_rows = mem.rearrange("(p t) w -> t p w", t=PACK)
+        page = []
+        for t, tag in enumerate(("x_bytes", "d_word_table", "x_byte_table", "x_word_table")):
+            page.append(keep.tile([P, U], F32, name="page%d" % t, tag=tag, align_bytes=64))
+            nc.sync.dma_start(out=page[t][:], in_=mem_rows[t])
+
+        pairs = [keep.tile([P, 2, HALF, 2], BF16, name="pairs%d" % c, align_bytes=64) for c in range(2)]
+        h_banks = []
+        for t in range(PACK):
+            h_ps = psum.tile([P, S], F32, name="h_ps%d" % t, tag="bank%d" % (4 + t))
+            nc.tensor.matmul_mx(out=h_ps[:], lhsT=d_dealt[:, t * P:(t + 1) * P].bitcast(FP8X4),
+                                lhsT_scale=scale_rows[:, t * P:(t + 1) * P],
+                                rhs=x_picked[:].bitcast(FP8X4), rhs_scale=scale_rows[:, H:H + S],
+                                start=True, stop=True)
+            h_banks.append(h_ps)
+        w_raw = keep.tile([P, PACK, N], F32, name="w_raw", tag="x_picked", align_bytes=64)
+        nc.sync.dma_start(out=w_raw[:], in_=w1.rearrange("(p j) n -> p j n", j=PACK))
+
+        for t in range(PACK):
+            h_ps = h_banks[t]
+            th = keep.tile([P, S], F32, name="th%d" % t)
+            diff = keep.tile([P, S], F32, name="diff%d" % t)
+            if t < 2:
+                old = keep.tile([P, S], F32, name="old%d" % t)[:]
+                step = keep.tile([P, S], F32, name="step%d" % t)[:]
+            else:
+                old = pairs[1][:, t - 2].rearrange("p w e -> p (w e)").bitcast(F32)[:, 0:S]
+                step = pairs[0][:, t - 2].rearrange("p w e -> p (w e)").bitcast(F32)[:, 0:S]
+            new = keep.tile([P, S], F32, name="new%d" % t)
+            nc.scalar.activation(out=th[:], in_=h_ps[:], func=ACT.Tanh, scale=0.03125)
+            nc.scalar.activation(out=old, in_=page[t][:].indirect(n1_sb[:]), func=ACT.Copy)
+            nc.vector.scalar_tensor_tensor(out=diff[:], in0=h_ps[:], scalar=0.0625, in1=old, op0=ALU.mult, op1=ALU.subtract)
+            nc.vector.scalar_tensor_tensor(out=step, in0=th[:], scalar=1.0, in1=diff[:], op0=ALU.add, op1=ALU.mult)
+            nc.vector.scalar_tensor_tensor(out=new[:], in0=step, scalar=0.5, in1=old, op0=ALU.mult, op1=ALU.add)
+            nc.scalar.activation(out=page[t][:].indirect(n1_sb[:]), in_=new[:], func=ACT.Copy)
+        for t in range(PACK):
+            for c in range(2):
+                nc.vector.tensor_scalar(out=pairs[c][:, t // 2, :, t % 2], in0=page[t][:, c * HALF:(c + 1) * HALF],
+                                        scalar1=gn_sb[:, t:t + 1], scalar2=None, op0=ALU.mult)
+
+        w_codes = keep.tile([P, N], U32, name="w_codes", align_bytes=64)
+        w_scales = keep.tile([P, N], U8, name="w_scales", align_bytes=64)
+
+        def quantise_weights(cols, name, tag):
+            width = cols.stop - cols.start
+            w_bf = keep.tile([P, width, PACK], BF16, name=name, tag=tag, align_bytes=64)
+            nc.vector.tensor_copy(out=w_bf[:].rearrange("p (c i) j -> p c j i", i=4),
+                                  in_=w_raw[:, :, cols].rearrange("p j (c i) -> p c j i", i=4))
+            nc.vector.quantize_mx(out=w_codes[:, cols].bitcast(FP8X4), scales=w_scales[:, cols],
+                                  in_=w_bf[:].rearrange("p n j -> p (n j)"))
+
+        quantise_weights(slice(0, P), "w_bf_first", "w_bf_first")
+        z_codes = []
+        z_scales = []
+        for c in range(2):
+            z_bf = keep.tile([P, HALF * PACK], BF16, name="z_bf%d" % c, align_bytes=64)
+            src = pairs[c][:].rearrange("p u w e -> p u (w e)")
+            nc.vector.tensor_copy(out=z_bf[:].bitcast(I32).rearrange("p (w u) -> p w u", u=2),
+                                  in_=src.bitcast(I32).rearrange("p u w -> p w u"))
+            codes = keep.tile([P, HALF], U32, name="z_codes%d" % c, align_bytes=64)
+            scales = keep.tile([P, HALF], U8, name="z_scales%d" % c, align_bytes=64)
+            nc.vector.quantize_mx(out=codes[:].bitcast(FP8X4), scales=scales[:], in_=z_bf[:])
+            z_codes.append(codes)
+            z_scales.append(scales)
+        quantise_weights(slice(P, N), "w_bf_rest", "z_bf1")
+
+        banks = []
+        recips = []
+        for m in range(N // P):
+            recip = keep.tile([P, U], F32, name="recip%d" % m)
+            recips.append(recip)
+            for c in range(2):
+                cols = slice(c * HALF, (c + 1) * HALF)
+                h2 = psum.tile([P, HALF], F32, name="h2_%d_%d" % (m, c), tag="bank%d" % (2 * m + c))
+                nc.tensor.matmul_mx(out=h2[:], lhsT=w_codes[:, m * P:(m + 1) * P].bitcast(FP8X4),
+                                    lhsT_scale=w_scales[:, m * P:(m + 1) * P],
+                                    rhs=z_codes[c][:].bitcast(FP8X4), rhs_scale=z_scales[c][:], start=True, stop=True)
+                banks.append(h2)
+                size = keep.tile([P, HALF], F32, name="size%d_%d" % (m, c))
+                root = keep.tile([P, HALF], F32, name="root%d_%d" % (m, c))
+                nc.scalar.activation(out=size[:], in_=h2[:], func=ACT.Abs)
+                nc.scalar.activation(out=root[:], in_=size[:], func=ACT.Abs_reciprocal_sqrt, bias=0.5)
+                square = nc.vector if m == 0 else nc.gpsimd
+                square.tensor_tensor(out=recip[:, cols], in0=root[:], in1=root[:], op=ALU.mult)
+        for m in range(N // P):
+            recip = recips[m]
+            for c in range(2):
+                cols = slice(c * HALF, (c + 1) * HALF)
+                picked = keep.tile([P, HALF], F32, name="picked%d_%d" % (m, c))
+                res = keep.tile([P, HALF], F32, name="res%d_%d" % (m, c))
+                looked_up = recip[:].indirect(n2_sb[:, c * HALF // 16:(c + 1) * HALF // 16])
+                if 2 * m + c < 5:
+                    nc.vector.tensor_copy(picked[:], looked_up)
+                else:
+                    nc.scalar.activation(out=picked[:], in_=looked_up, func=ACT.Copy)
+                nc.vector.tensor_tensor(out=res[:], in0=banks[2 * m + c][:], in1=picked[:], op=ALU.mult)
+                nc.sync.dma_start(out=out[m * P:(m + 1) * P, cols], in_=res[:])

@@ -33,10 +33,11 @@ def tile_picked_hpqpagetnorm_none_p_kernel(tc, x_words, x_scales, d_words, d_sca
 
         d_byte_table = keep.tile([P, G], U8, name="d_byte_table", align_bytes=64)
         x_byte_table = keep.tile([P, T], U8, name="x_byte_table", align_bytes=64)
-        nc.vector.memset(d_byte_table[:].bitcast(I32), 0)
-        nc.gpsimd.memset(x_byte_table[:].bitcast(I32), 0)
-        nc.scalar.dma_start(out=d_byte_table[0:P:8, :].bitcast(I32), in_=d_scales[0].bitcast(I32))
-        nc.scalar.dma_start(out=x_byte_table[0:P:8, :].bitcast(I32), in_=x_scales[0].bitcast(I32))
+        nc.gpsimd.memset(d_byte_table[:].bitcast(I32), 0)
+        nc.gpsimd.memset(x_byte_table[:, 0:T // 2].bitcast(I32), 0)
+        nc.vector.memset(x_byte_table[:, T // 2:T].bitcast(I32), 0)
+        nc.sync.dma_start(out=d_byte_table[0:P:8, :].bitcast(I32), in_=d_scales[0].bitcast(I32))
+        nc.sync.dma_start(out=x_byte_table[0:P:8, :].bitcast(I32), in_=x_scales[0].bitcast(I32))
 
         d_word_table = keep.tile([P, G], I32, name="d_word_table", align_bytes=64)
         x_word_table = keep.tile([P, T], I32, name="x_word_table", align_bytes=64)
@@ -49,18 +50,15 @@ def tile_picked_hpqpagetnorm_none_p_kernel(tc, x_words, x_scales, d_words, d_sca
         gn_sb = keep.tile([P, PACK], F32, name="gn_sb")
         nc.gpsimd.dma_start(out=gn_sb[:], in_=gn.rearrange("(p t) o -> p (t o)", t=PACK))
 
-        d_bytes = keep.tile([P, H], U8, name="d_bytes", align_bytes=64)
-        x_bytes = keep.tile([P, S], U8, name="x_bytes", align_bytes=64)
-        dealt_bytes = keep.tile([P, H + S], U8, name="dealt_bytes", align_bytes=64)
+        picked_bytes = keep.tile([P, H + S], U8, name="picked_bytes", align_bytes=64)
         scale_rows = keep.tile([P, H + S], U8, name="scale_rows", align_bytes=64)
-        nc.vector.tensor_copy(d_bytes[:], d_byte_table[:].indirect(k1_sb[:]))
-        nc.vector.tensor_copy(x_bytes[:], x_byte_table[:].indirect(offs_sb[:]))
-        nc.vector.tensor_copy(out=dealt_bytes[:, 0:H].rearrange("p (t m) -> p t m", t=PACK),
-                              in_=d_bytes[:].rearrange("p (m t) -> p t m", t=PACK))
-        nc.vector.tensor_copy(out=dealt_bytes[:, H:H + S].bitcast(I32), in_=x_bytes[:].bitcast(I32))
-        nc.vector.tensor_copy(out=scale_rows[:].bitcast(I32), in_=dealt_bytes[:].bitcast(I32))
-        for b in range(1, 4):
-            nc.scalar.dma_start(out=scale_rows[b:P:32, :].bitcast(I32), in_=dealt_bytes[8 * b:P:32, :].bitcast(I32))
+        d_scale_rows = keep.tile([P, H], U8, name="d_scale_rows", align_bytes=64)
+        nc.gpsimd.memset(scale_rows[:].bitcast(I32), 0)
+        nc.vector.tensor_copy(picked_bytes[:, 0:H], d_byte_table[:].indirect(k1_sb[:]))
+        nc.vector.tensor_copy(picked_bytes[:, H:H + S], x_byte_table[:].indirect(offs_sb[:]))
+        for b in range(4):
+            queue = nc.scalar if b % 2 else nc.sync
+            queue.dma_start(out=scale_rows[b:P:32, :].bitcast(I32), in_=picked_bytes[8 * b:P:32, :].bitcast(I32))
 
         d_picked = keep.tile([P, H], U32, name="d_picked", tag="x_byte_table", align_bytes=64)
         d_dealt = keep.tile([P, H], U32, name="d_dealt", align_bytes=64)
@@ -69,10 +67,12 @@ def tile_picked_hpqpagetnorm_none_p_kernel(tc, x_words, x_scales, d_words, d_sca
         nc.vector.tensor_copy(out=d_dealt[:].rearrange("p (t m) -> p t m", t=PACK),
                               in_=d_picked[:].rearrange("p (m t) -> p t m", t=PACK))
         nc.vector.tensor_copy(x_picked[:], x_word_table[:].bitcast(U32).indirect(offs_sb[:]))
+        for t in range(PACK):
+            nc.vector.tensor_copy(out=d_scale_rows[:, t * P:(t + 1) * P], in_=scale_rows[:, t:H:PACK])
 
         mem_rows = mem.rearrange("(p t) w -> t p w", t=PACK)
         page = []
-        for t, tag in enumerate(("x_bytes", "d_word_table", "x_byte_table", "x_word_table")):
+        for t, tag in enumerate(("d_word_table", "x_byte_table", "x_word_table", "picked_bytes")):
             page.append(keep.tile([P, U], F32, name="page%d" % t, tag=tag, align_bytes=64))
             nc.sync.dma_start(out=page[t][:], in_=mem_rows[t])
 
@@ -81,7 +81,7 @@ def tile_picked_hpqpagetnorm_none_p_kernel(tc, x_words, x_scales, d_words, d_sca
         for t in range(PACK):
             h_ps = psum.tile([P, S], F32, name="h_ps%d" % t, tag="bank%d" % (4 + t))
             nc.tensor.matmul_mx(out=h_ps[:], lhsT=d_dealt[:, t * P:(t + 1) * P].bitcast(FP8X4),
-                                lhsT_scale=scale_rows[:, t * P:(t + 1) * P],
+                                lhsT_scale=d_scale_rows[:, t * P:(t + 1) * P],
                                 rhs=x_picked[:].bitcast(FP8X4), rhs_scale=scale_rows[:, H:H + S],
                                 start=True, stop=True)
             h_banks.append(h_ps)
@@ -127,8 +127,9 @@ def tile_picked_hpqpagetnorm_none_p_kernel(tc, x_words, x_scales, d_words, d_sca
         for c in range(2):
             z_bf = keep.tile([P, HALF * PACK], BF16, name="z_bf%d" % c, align_bytes=64)
             src = pairs[c][:].rearrange("p u w e -> p u (w e)")
-            nc.vector.tensor_copy(out=z_bf[:].bitcast(I32).rearrange("p (w u) -> p w u", u=2),
-                                  in_=src.bitcast(I32).rearrange("p u w -> p w u"))
+            weave = nc.vector.tensor_copy if c == 0 else nc.scalar.copy
+            weave(out=z_bf[:].bitcast(U32).rearrange("p (w u) -> p w u", u=2),
+                  in_=src.bitcast(U32).rearrange("p u w -> p w u"))
             codes = keep.tile([P, HALF], U32, name="z_codes%d" % c, align_bytes=64)
             scales = keep.tile([P, HALF], U8, name="z_scales%d" % c, align_bytes=64)
             nc.vector.quantize_mx(out=codes[:].bitcast(FP8X4), scales=scales[:], in_=z_bf[:])
@@ -152,18 +153,22 @@ def tile_picked_hpqpagetnorm_none_p_kernel(tc, x_words, x_scales, d_words, d_sca
                 root = keep.tile([P, HALF], F32, name="root%d_%d" % (m, c))
                 nc.scalar.activation(out=size[:], in_=h2[:], func=ACT.Abs)
                 nc.scalar.activation(out=root[:], in_=size[:], func=ACT.Abs_reciprocal_sqrt, bias=0.5)
-                square = nc.vector if m == 0 else nc.gpsimd
+                square = nc.vector if 2 * m + c in (0, 1, 7) else nc.gpsimd
                 square.tensor_tensor(out=recip[:, cols], in0=root[:], in1=root[:], op=ALU.mult)
         for m in range(N // P):
-            recip = recips[m]
             for c in range(2):
-                cols = slice(c * HALF, (c + 1) * HALF)
-                picked = keep.tile([P, HALF], F32, name="picked%d_%d" % (m, c))
-                res = keep.tile([P, HALF], F32, name="res%d_%d" % (m, c))
-                looked_up = recip[:].indirect(n2_sb[:, c * HALF // 16:(c + 1) * HALF // 16])
-                if 2 * m + c < 5:
-                    nc.vector.tensor_copy(picked[:], looked_up)
-                else:
-                    nc.scalar.activation(out=picked[:], in_=looked_up, func=ACT.Copy)
-                nc.vector.tensor_tensor(out=res[:], in0=banks[2 * m + c][:], in1=picked[:], op=ALU.mult)
-                nc.sync.dma_start(out=out[m * P:(m + 1) * P, cols], in_=res[:])
+                half = 2 * m + c
+                pieces = 2 if half == 7 else 1
+                width = HALF // pieces
+                for i in range(pieces):
+                    lo = c * HALF + i * width
+                    name = "%d_%d" % (half, i)
+                    picked = keep.tile([P, width], F32, name="picked" + name, tag="root3_1" if half == 4 else "picked" + name)
+                    res = keep.tile([P, width], F32, name="res" + name)
+                    looked_up = recips[m][:].indirect(n2_sb[:, lo // 16:(lo + width) // 16])
+                    if half < 5:
+                        nc.vector.tensor_copy(picked[:], looked_up)
+                    else:
+                        nc.scalar.activation(out=picked[:], in_=looked_up, func=ACT.Copy)
+                    nc.vector.tensor_tensor(out=res[:], in0=banks[half][:, i * width:(i + 1) * width], in1=picked[:], op=ALU.mult)
+                    nc.sync.dma_start(out=out[m * P:(m + 1) * P, lo:lo + width], in_=res[:])

@@ -60,7 +60,7 @@ def tile_picked_hpqpagetnorm_none_p_kernel(tc, x_words, x_scales, d_words, d_sca
             queue = nc.scalar if b % 2 else nc.sync
             queue.dma_start(out=scale_rows[b:P:32, :].bitcast(I32), in_=picked_bytes[8 * b:P:32, :].bitcast(I32))
 
-        d_picked = keep.tile([P, H], U32, name="d_picked", tag="x_byte_table", align_bytes=64)
+        d_picked = keep.tile([P, H], U32, name="d_picked", tag="d_byte_table", align_bytes=64)
         d_dealt = keep.tile([P, H], U32, name="d_dealt", align_bytes=64)
         x_picked = keep.tile([P, S], U32, name="x_picked", align_bytes=64)
         nc.vector.tensor_copy(d_picked[:], d_word_table[:].bitcast(U32).indirect(k1_sb[:]))
@@ -72,7 +72,7 @@ def tile_picked_hpqpagetnorm_none_p_kernel(tc, x_words, x_scales, d_words, d_sca
 
         mem_rows = mem.rearrange("(p t) w -> t p w", t=PACK)
         page = []
-        for t, tag in enumerate(("d_word_table", "x_byte_table", "x_word_table", "picked_bytes")):
+        for t, tag in enumerate(("x_byte_table", "d_word_table", "d_byte_table", "x_word_table")):
             page.append(keep.tile([P, U], F32, name="page%d" % t, tag=tag, align_bytes=64))
             nc.sync.dma_start(out=page[t][:], in_=mem_rows[t])
 
@@ -127,9 +127,13 @@ def tile_picked_hpqpagetnorm_none_p_kernel(tc, x_words, x_scales, d_words, d_sca
         for c in range(2):
             z_bf = keep.tile([P, HALF * PACK], BF16, name="z_bf%d" % c, align_bytes=64)
             src = pairs[c][:].rearrange("p u w e -> p u (w e)")
-            weave = nc.vector.tensor_copy if c == 0 else nc.scalar.copy
-            weave(out=z_bf[:].bitcast(U32).rearrange("p (w u) -> p w u", u=2),
-                  in_=src.bitcast(U32).rearrange("p u w -> p w u"))
+            woven = z_bf[:].bitcast(U32).rearrange("p (w u) -> p w u", u=2)
+            loose = src.bitcast(U32).rearrange("p u w -> p w u")
+            if c == 0:
+                nc.vector.tensor_copy(out=woven, in_=loose)
+            else:
+                nc.scalar.copy(out=woven[:, 0:HALF // 2], in_=loose[:, 0:HALF // 2])
+                nc.vector.tensor_copy(out=woven[:, HALF // 2:HALF], in_=loose[:, HALF // 2:HALF])
             codes = keep.tile([P, HALF], U32, name="z_codes%d" % c, align_bytes=64)
             scales = keep.tile([P, HALF], U8, name="z_scales%d" % c, align_bytes=64)
             nc.vector.quantize_mx(out=codes[:].bitcast(FP8X4), scales=scales[:], in_=z_bf[:])

@@ -47,8 +47,6 @@ def tile_picked_hpqpagetnorm_none_p_kernel(tc, x_words, x_scales, d_words, d_sca
         nc.sync.dma_start(n2_sb[:], n2)
         nc.sync.dma_start(out=d_word_table[:], in_=d_words[0].rearrange("p n t -> p (n t)").bitcast(I32))
         nc.sync.dma_start(out=x_word_table[:], in_=x_words[0].rearrange("p n t -> p (n t)").bitcast(I32))
-        gn_sb = keep.tile([P, PACK], F32, name="gn_sb")
-        nc.gpsimd.dma_start(out=gn_sb[:], in_=gn.rearrange("(p t) o -> p (t o)", t=PACK))
 
         picked_bytes = keep.tile([P, H + S], U8, name="picked_bytes", align_bytes=64)
         scale_rows = keep.tile([P, H + S], U8, name="scale_rows", align_bytes=64)
@@ -57,8 +55,7 @@ def tile_picked_hpqpagetnorm_none_p_kernel(tc, x_words, x_scales, d_words, d_sca
         nc.vector.tensor_copy(picked_bytes[:, 0:H], d_byte_table[:].indirect(k1_sb[:]))
         nc.vector.tensor_copy(picked_bytes[:, H:H + S], x_byte_table[:].indirect(offs_sb[:]))
         for b in range(4):
-            queue = nc.scalar if b % 2 else nc.sync
-            queue.dma_start(out=scale_rows[b:P:32, :].bitcast(I32), in_=picked_bytes[8 * b:P:32, :].bitcast(I32))
+            nc.sync.dma_start(out=scale_rows[b:P:32, :].bitcast(I32), in_=picked_bytes[8 * b:P:32, :].bitcast(I32))
 
         d_picked = keep.tile([P, H], U32, name="d_picked", tag="d_byte_table", align_bytes=64)
         d_dealt = keep.tile([P, H], U32, name="d_dealt", align_bytes=64)
@@ -75,6 +72,9 @@ def tile_picked_hpqpagetnorm_none_p_kernel(tc, x_words, x_scales, d_words, d_sca
         for t, tag in enumerate(("x_byte_table", "d_word_table", "d_byte_table", "x_word_table")):
             page.append(keep.tile([P, U], F32, name="page%d" % t, tag=tag, align_bytes=64))
             nc.sync.dma_start(out=page[t][:], in_=mem_rows[t])
+
+        gn_sb = keep.tile([P, PACK], F32, name="gn_sb", tag="picked_bytes", align_bytes=64)
+        nc.sync.dma_start(out=gn_sb[:], in_=gn.rearrange("(p t) o -> p (t o)", t=PACK))
 
         pairs = [keep.tile([P, 2, HALF, 2], BF16, name="pairs%d" % c, align_bytes=64) for c in range(2)]
         h_banks = []
@@ -105,6 +105,8 @@ def tile_picked_hpqpagetnorm_none_p_kernel(tc, x_words, x_scales, d_words, d_sca
             nc.vector.scalar_tensor_tensor(out=step, in0=th[:], scalar=1.0, in1=diff[:], op0=ALU.add, op1=ALU.mult)
             nc.vector.scalar_tensor_tensor(out=new[:], in0=step, scalar=0.5, in1=old, op0=ALU.mult, op1=ALU.add)
             nc.scalar.activation(out=page[t][:].indirect(n1_sb[:]), in_=new[:], func=ACT.Copy)
+        warm = keep.tile([P, 1], F32, name="warm", tag="new3")
+        nc.scalar.activation(out=warm[:], in_=gn_sb[:, 0:1], func=ACT.Abs_reciprocal_sqrt, bias=0.5)
         for t in range(PACK):
             for c in range(2):
                 nc.vector.tensor_scalar(out=pairs[c][:, t // 2, :, t % 2], in0=page[t][:, c * HALF:(c + 1) * HALF],
@@ -144,6 +146,8 @@ def tile_picked_hpqpagetnorm_none_p_kernel(tc, x_words, x_scales, d_words, d_sca
         banks = []
         recips = []
         for m in range(N // P):
+            size = keep.tile([P, U], F32, name="size%d" % m)
+            root = keep.tile([P, U], F32, name="root%d" % m)
             recip = keep.tile([P, U], F32, name="recip%d" % m)
             recips.append(recip)
             for c in range(2):
@@ -153,12 +157,24 @@ def tile_picked_hpqpagetnorm_none_p_kernel(tc, x_words, x_scales, d_words, d_sca
                                     lhsT_scale=w_scales[:, m * P:(m + 1) * P],
                                     rhs=z_codes[c][:].bitcast(FP8X4), rhs_scale=z_scales[c][:], start=True, stop=True)
                 banks.append(h2)
-                size = keep.tile([P, HALF], F32, name="size%d_%d" % (m, c))
-                root = keep.tile([P, HALF], F32, name="root%d_%d" % (m, c))
-                nc.scalar.activation(out=size[:], in_=h2[:], func=ACT.Abs)
+                nc.scalar.activation(out=size[:, cols], in_=h2[:], func=ACT.Abs)
+                if m == 0:
+                    nc.scalar.activation(out=root[:, cols], in_=size[:, cols], func=ACT.Abs_reciprocal_sqrt, bias=0.5)
+                    nc.vector.tensor_tensor(out=recip[:, cols], in0=root[:, cols], in1=root[:, cols], op=ALU.mult)
+            if m > 0:
                 nc.scalar.activation(out=root[:], in_=size[:], func=ACT.Abs_reciprocal_sqrt, bias=0.5)
-                square = nc.vector if 2 * m + c in (0, 1, 7) else nc.gpsimd
-                square.tensor_tensor(out=recip[:, cols], in0=root[:], in1=root[:], op=ALU.mult)
+                if m == 1:
+                    nc.vector.tensor_tensor(out=recip[:], in0=root[:], in1=root[:], op=ALU.mult)
+                else:
+                    nc.scalar.activation(out=recip[:], in_=root[:], func=ACT.Square)
+
+        def look_up(engine, picked, m, lo, width):
+            looked_up = recips[m][:].indirect(n2_sb[:, lo // 16:(lo + width) // 16])
+            if engine == "vector":
+                nc.vector.tensor_copy(picked, looked_up)
+            else:
+                nc.scalar.activation(out=picked, in_=looked_up, func=ACT.Copy)
+
         for m in range(N // P):
             for c in range(2):
                 half = 2 * m + c
@@ -167,12 +183,8 @@ def tile_picked_hpqpagetnorm_none_p_kernel(tc, x_words, x_scales, d_words, d_sca
                 for i in range(pieces):
                     lo = c * HALF + i * width
                     name = "%d_%d" % (half, i)
-                    picked = keep.tile([P, width], F32, name="picked" + name, tag="root3_1" if half == 4 else "picked" + name)
+                    picked = keep.tile([P, width], F32, name="picked" + name)
                     res = keep.tile([P, width], F32, name="res" + name)
-                    looked_up = recips[m][:].indirect(n2_sb[:, lo // 16:(lo + width) // 16])
-                    if half < 5:
-                        nc.vector.tensor_copy(picked[:], looked_up)
-                    else:
-                        nc.scalar.activation(out=picked[:], in_=looked_up, func=ACT.Copy)
+                    look_up("vector" if half < 5 else "scalar", picked[:], m, lo, width)
                     nc.vector.tensor_tensor(out=res[:], in0=banks[half][:, i * width:(i + 1) * width], in1=picked[:], op=ALU.mult)
                     nc.sync.dma_start(out=out[m * P:(m + 1) * P, lo:lo + width], in_=res[:])

from contextlib import ExitStack

import concourse.mybir as mybir

F32 = mybir.dt.float32
BF16 = mybir.dt.bfloat16
I32 = mybir.dt.int32
U32 = mybir.dt.uint32
U16 = mybir.dt.uint16
U8 = mybir.dt.uint8
FP8X4 = mybir.dt.float8_e4m3fn_x4
ACT = mybir.ActivationFunctionType
ALU = mybir.AluOpType

P = 128
PACK = 4
K, T, S, N, G, H, U = 512, 2048, 256, 512, 2048, 512, 1024
HALF = U // 2
FLOPS = 2 * K * H * S + 2 * H * N * U


def tile_picked_hpqpagetnorm_none_p_kernel(tc, x_words, x_scales, d_words, d_scales, mem, gn, w1, offs, k1, n1, n2, out):
    nc = tc.nc
    with ExitStack() as ctx:
        lists = ctx.enter_context(tc.tile_pool(name="lists", bufs=1))
        keep = ctx.enter_context(tc.tile_pool(name="keep", bufs=1))
        psum = ctx.enter_context(tc.psum_pool(name="psum", bufs=1))

        k1_sb = lists.tile([P, H // 16], U16, name="k1_sb")
        offs_sb = lists.tile([P, S // 16], U16, name="offs_sb")
        n1_sb = lists.tile([P, S // 16], U16, name="n1_sb")
        n2_sb = lists.tile([P, U // 16], U16, name="n2_sb")

        d_byte_table = keep.tile([P, G], U8, name="d_byte_table", align_bytes=64)
        x_byte_table = keep.tile([P, T], U8, name="x_byte_table", align_bytes=64)
        nc.gpsimd.memset(d_byte_table[:].bitcast(I32), 0)
        nc.gpsimd.memset(x_byte_table[:, 0:T // 2].bitcast(I32), 0)
        nc.vector.memset(x_byte_table[:, T // 2:T].bitcast(I32), 0)
        nc.sync.dma_start(out=d_byte_table[0:P:8, :].bitcast(I32), in_=d_scales[0].bitcast(I32))
        nc.sync.dma_start(out=x_byte_table[0:P:8, :].bitcast(I32), in_=x_scales[0].bitcast(I32))

        d_word_table = keep.tile([P, G], I32, name="d_word_table", align_bytes=64)
        x_word_table = keep.tile([P, T], I32, name="x_word_table", align_bytes=64)
        nc.sync.dma_start(k1_sb[:], k1)
        nc.sync.dma_start(offs_sb[:], offs)
        nc.sync.dma_start(n1_sb[:], n1)
        nc.sync.dma_start(n2_sb[:], n2)
        nc.sync.dma_start(out=d_word_table[:], in_=d_words[0].rearrange("p n t -> p (n t)").bitcast(I32))
        nc.sync.dma_start(out=x_word_table[:], in_=x_words[0].rearrange("p n t -> p (n t)").bitcast(I32))

        picked_bytes = keep.tile([P, H + S], U8, name="picked_bytes", align_bytes=64)
        scale_rows = keep.tile([P, H + S], U8, name="scale_rows", align_bytes=64)
        d_scale_rows = keep.tile([P, H], U8, name="d_scale_rows", align_bytes=64)
        nc.gpsimd.memset(scale_rows[:].bitcast(I32), 0)
        nc.vector.tensor_copy(picked_bytes[:, 0:H], d_byte_table[:].indirect(k1_sb[:]))
        nc.vector.tensor_copy(picked_bytes[:, H:H + S], x_byte_table[:].indirect(offs_sb[:]))
        for b in range(4):
            nc.sync.dma_start(out=scale_rows[b:P:32, :].bitcast(I32), in_=picked_bytes[8 * b:P:32, :].bitcast(I32))

        d_picked = keep.tile([P, H], U32, name="d_picked", tag="d_byte_table", align_bytes=64)
        d_dealt = keep.tile([P, H], U32, name="d_dealt", align_bytes=64)
        x_picked = keep.tile([P, S], U32, name="x_picked", align_bytes=64)
        nc.vector.tensor_copy(d_picked[:], d_word_table[:].bitcast(U32).indirect(k1_sb[:]))
        nc.vector.tensor_copy(out=d_dealt[:].rearrange("p (t m) -> p t m", t=PACK),
                              in_=d_picked[:].rearrange("p (m t) -> p t m", t=PACK))
        nc.vector.tensor_copy(x_picked[:], x_word_table[:].bitcast(U32).indirect(offs_sb[:]))
        for t in range(PACK):
            nc.vector.tensor_copy(out=d_scale_rows[:, t * P:(t + 1) * P], in_=scale_rows[:, t:H:PACK])

        mem_rows = mem.rearrange("(p t) w -> t p w", t=PACK)
        page = []
        for t, tag in enumerate(("x_byte_table", "d_word_table", "d_byte_table", "x_word_table")):
            page.append(keep.tile([P, U], F32, name="page%d" % t, tag=tag, align_bytes=64))
            nc.sync.dma_start(out=page[t][:], in_=mem_rows[t])

        gn_sb = keep.tile([P, PACK], F32, name="gn_sb", tag="picked_bytes", align_bytes=64)
        nc.sync.dma_start(out=gn_sb[:], in_=gn.rearrange("(p t) o -> p (t o)", t=PACK))

        pairs = [keep.tile([P, 2, HALF, 2], BF16, name="pairs%d" % c, align_bytes=64) for c in range(2)]
        h_banks = []
        for t in range(PACK):
            h_ps = psum.tile([P, S], F32, name="h_ps%d" % t, tag="bank%d" % (4 + t))
            nc.tensor.matmul_mx(out=h_ps[:], lhsT=d_dealt[:, t * P:(t + 1) * P].bitcast(FP8X4),
                                lhsT_scale=d_scale_rows[:, t * P:(t + 1) * P],
                                rhs=x_picked[:].bitcast(FP8X4), rhs_scale=scale_rows[:, H:H + S],
                                start=True, stop=True)
            h_banks.append(h_ps)
        w_raw = keep.tile([P, PACK, N], F32, name="w_raw", tag="x_picked", align_bytes=64)
        nc.sync.dma_start(out=w_raw[:], in_=w1.rearrange("(p j) n -> p j n", j=PACK))

        for t in range(PACK):
            h_ps = h_banks[t]
            th = keep.tile([P, S], F32, name="th%d" % t)
            diff = keep.tile([P, S], F32, name="diff%d" % t)
            if t < 2:
                old = keep.tile([P, S], F32, name="old%d" % t)[:]
                step = keep.tile([P, S], F32, name="step%d" % t)[:]
            else:
                old = pairs[1][:, t - 2].rearrange("p w e -> p (w e)").bitcast(F32)[:, 0:S]
                step = pairs[0][:, t - 2].rearrange("p w e -> p (w e)").bitcast(F32)[:, 0:S]
            new = keep.tile([P, S], F32, name="new%d" % t)
            nc.scalar.activation(out=th[:], in_=h_ps[:], func=ACT.Tanh, scale=0.03125)
            nc.scalar.activation(out=old, in_=page[t][:].indirect(n1_sb[:]), func=ACT.Copy)
            nc.vector.scalar_tensor_tensor(out=diff[:], in0=h_ps[:], scalar=0.0625, in1=old, op0=ALU.mult, op1=ALU.subtract)
            nc.vector.scalar_tensor_tensor(out=step, in0=th[:], scalar=1.0, in1=diff[:], op0=ALU.add, op1=ALU.mult)
            nc.vector.scalar_tensor_tensor(out=new[:], in0=step, scalar=0.5, in1=old, op0=ALU.mult, op1=ALU.add)
            nc.scalar.activation(out=page[t][:].indirect(n1_sb[:]), in_=new[:], func=ACT.Copy)
        warm = keep.tile([P, 1], F32, name="warm", tag="new3")
        nc.scalar.activation(out=warm[:], in_=gn_sb[:, 0:1], func=ACT.Abs_reciprocal_sqrt, bias=0.5)
        for t in range(PACK):
            for c in range(2):
                nc.vector.tensor_scalar(out=pairs[c][:, t // 2, :, t % 2], in0=page[t][:, c * HALF:(c + 1) * HALF],
                                        scalar1=gn_sb[:, t:t + 1], scalar2=None, op0=ALU.mult)

        w_codes = keep.tile([P, N], U32, name="w_codes", align_bytes=64)
        w_scales = keep.tile([P, N], U8, name="w_scales", align_bytes=64)

        def quantise_weights(cols, name, tag):
            width = cols.stop - cols.start
            w_bf = keep.tile([P, width, PACK], BF16, name=name, tag=tag, align_bytes=64)
            nc.vector.tensor_copy(out=w_bf[:].rearrange("p (c i) j -> p c j i", i=4),
                                  in_=w_raw[:, :, cols].rearrange("p j (c i) -> p c j i", i=4))
            nc.vector.quantize_mx(out=w_codes[:, cols].bitcast(FP8X4), scales=w_scales[:, cols],
                                  in_=w_bf[:].rearrange("p n j -> p (n j)"))

        quantise_weights(slice(0, P), "w_bf_first", "w_bf_first")
        z_codes = []
        z_scales = []
        for c in range(2):
            z_bf = keep.tile([P, HALF * PACK], BF16, name="z_bf%d" % c, align_bytes=64)
            src = pairs[c][:].rearrange("p u w e -> p u (w e)")
            woven = z_bf[:].bitcast(U32).rearrange("p (w u) -> p w u", u=2)
            loose = src.bitcast(U32).rearrange("p u w -> p w u")
            if c == 0:
                nc.vector.tensor_copy(out=woven, in_=loose)
            else:
                nc.scalar.copy(out=woven[:, 0:HALF // 2], in_=loose[:, 0:HALF // 2])
                nc.vector.tensor_copy(out=woven[:, HALF // 2:HALF], in_=loose[:, HALF // 2:HALF])
            codes = keep.tile([P, HALF], U32, name="z_codes%d" % c, align_bytes=64)
            scales = keep.tile([P, HALF], U8, name="z_scales%d" % c, align_bytes=64)
            nc.vector.quantize_mx(out=codes[:].bitcast(FP8X4), scales=scales[:], in_=z_bf[:])
            z_codes.append(codes)
            z_scales.append(scales)
        quantise_weights(slice(P, N), "w_bf_rest", "z_bf1")

        banks = []
        recips = []
        for m in range(N // P):
            size = keep.tile([P, U], F32, name="size%d" % m)
            root = keep.tile([P, U], F32, name="root%d" % m)
            recip = keep.tile([P, U], F32, name="recip%d" % m)
            recips.append(recip)
            for c in range(2):
                cols = slice(c * HALF, (c + 1) * HALF)
                h2 = psum.tile([P, HALF], F32, name="h2_%d_%d" % (m, c), tag="bank%d" % (2 * m + c))
                nc.tensor.matmul_mx(out=h2[:], lhsT=w_codes[:, m * P:(m + 1) * P].bitcast(FP8X4),
                                    lhsT_scale=w_scales[:, m * P:(m + 1) * P],
                                    rhs=z_codes[c][:].bitcast(FP8X4), rhs_scale=z_scales[c][:], start=True, stop=True)
                banks.append(h2)
                nc.scalar.activation(out=size[:, cols], in_=h2[:], func=ACT.Abs)
                if m == 0:
                    nc.scalar.activation(out=root[:, cols], in_=size[:, cols], func=ACT.Abs_reciprocal_sqrt, bias=0.5)
                    nc.vector.tensor_tensor(out=recip[:, cols], in0=root[:, cols], in1=root[:, cols], op=ALU.mult)
            if m > 0:
                nc.scalar.activation(out=root[:], in_=size[:], func=ACT.Abs_reciprocal_sqrt, bias=0.5)
                if m == 1:
                    nc.vector.tensor_tensor(out=recip[:], in0=root[:], in1=root[:], op=ALU.mult)
                else:
                    nc.scalar.activation(out=recip[:], in_=root[:], func=ACT.Square)

        def look_up(engine, picked, m, lo, width):
            looked_up = recips[m][:].indirect(n2_sb[:, lo // 16:(lo + width) // 16])
            if engine == "vector":
                nc.vector.tensor_copy(picked, looked_up)
            else:
                nc.scalar.activation(out=picked, in_=looked_up, func=ACT.Copy)

        for m in range(N // P):
            for c in range(2):
                half = 2 * m + c
                pieces = 2 if half == 7 else 1
                width = HALF // pieces
                for i in range(pieces):
                    lo = c * HALF + i * width
                    name = "%d_%d" % (half, i)
                    picked = keep.tile([P, width], F32, name="picked" + name)
                    res = keep.tile([P, width], F32, name="res" + name)
                    look_up("vector" if half < 5 else "scalar", picked[:], m, lo, width)
                    nc.vector.tensor_tensor(out=res[:], in0=banks[half][:, i * width:(i + 1) * width], in1=picked[:], op=ALU.mult)
                    nc.sync.dma_start(out=out[m * P:(m + 1) * P, lo:lo + width], in_=res[:])
